import numpy as np
import ml_dtypes


def mxq(x, axis, fmt="e4m3"):
    dtype, down = {"e4m3": (ml_dtypes.float8_e4m3fn, 7), "e5m2": (ml_dtypes.float8_e5m2, 14)}[fmt]
    v = np.moveaxis(np.asarray(x, np.float32).astype(ml_dtypes.bfloat16).astype(np.float64), axis, -1)
    blocks = v.reshape(v.shape[:-1] + (-1, 32))
    amax = np.abs(blocks).max(-1, keepdims=True)
    byte = np.maximum(np.where(amax > 0, np.frexp(amax)[1] - 1 + 127, 0) - down, 1)
    scale = np.exp2(byte - 127.0)
    codes = (blocks / scale).astype(np.float32).astype(dtype).astype(np.float64)
    return np.moveaxis((codes * scale).reshape(v.shape), -1, axis)


WIDE = False


def mx_kscale(k):
    if not WIDE:
        return np.ones(k)
    levels = np.array([10, -10, 5, -5, 0])
    if k % 512:
        return np.exp2(np.random.permutation(np.resize(levels, k // 32))).repeat(32)
    a = np.empty((k // 512, 16))
    for p in range(k // 512):
        a[p, :8] = np.random.permutation(np.resize(levels, 8))
        for g in range(8):
            far = levels[np.abs(levels - a[p, g]) >= 10]
            a[p, g + 8] = far[np.random.randint(len(far))]
    return np.exp2(a.ravel()).repeat(32)


def f64(x):
    return np.asarray(x).astype(np.float64)


def striped(idx):
    return np.tile(np.asarray(idx).reshape(-1, 16).T, (8, 1)).astype(np.uint16)


def unstriped(offs):
    return offs[:16].T.reshape(-1).astype(np.int64)


E2M1 = np.array([0.0, 0.5, 1.0, 1.5, 2.0, 3.0, 4.0, 6.0, -0.0, -0.5, -1.0, -1.5, -2.0, -3.0, -4.0, -6.0])


def pack_weight(w, fmt):
    k, n = w.shape
    w = f64(np.asarray(w, np.float32).astype(ml_dtypes.bfloat16)).reshape(k // 32, 32, n)
    amax = np.abs(w).max(1)
    if fmt == "e4m3":
        byte = np.frexp(amax)[1] - 1 + 127 - 7
    else:
        mant, ex = np.frexp(amax / 6.0)
        byte = np.where(mant > 0.5, ex, ex - 1) + 127
    byte = np.clip(np.where(amax > 0, byte, 1), 1, 254)
    scaled = (w * np.exp2(127.0 - byte)[:, None, :]).reshape(k, n).astype(np.float32)
    by_word = np.ascontiguousarray(scaled.reshape(k // 512, 128, 4, n).transpose(0, 1, 3, 2))
    if fmt == "e4m3":
        words = by_word.astype(ml_dtypes.float8_e4m3fn).view(np.uint8)
    else:
        c = by_word.astype(ml_dtypes.float4_e2m1fn).view(np.uint8) & 0xF
        words = (c[..., 0::2] | (c[..., 1::2] << 4)).reshape(k // 512, 128, 2 * n)
    return np.ascontiguousarray(words), np.ascontiguousarray(byte.astype(np.uint8).reshape(k // 512, 16, n))


def unpack_weight(words, scales, fmt):
    g, _, n = scales.shape
    words = np.ascontiguousarray(words).reshape(g, 128, n, -1)
    if fmt == "e4m3":
        vals = words.view(ml_dtypes.float8_e4m3fn).astype(np.float64)
    else:
        nib = np.empty((g, 128, n, 4), np.uint8)
        nib[..., 0::2] = words & 0xF
        nib[..., 1::2] = words >> 4
        vals = E2M1[nib]
    vals = vals * np.repeat(np.exp2(scales.astype(np.float64) - 127.0), 8, axis=1)[..., None]
    return vals.transpose(0, 1, 3, 2).reshape(g * 512, n)


B, N, T, D, NQ = 1, 512, 4096, 512, 256


def setup_inputs():
    n = np.random.standard_normal
    idx = np.sort(np.random.permutation(T)[:B * N].reshape(B, N), axis=1).reshape(-1)
    s = mx_kscale(D)[:, None]
    kp = pack_weight(n((D, T)) / s, "e4m3")
    return {
        "qT": (n((B, D, NQ)) * s * (1.00 / np.sqrt(D))).astype(np.float32),
        "k_words": kp[0],
        "k_scales": kp[1],
        "offs": striped(idx),
    }


def reference(qT, k_words, k_scales, offs):
    idx = unstriped(offs)
    pick = lambda x, which: x[:, which].reshape(x.shape[0], B, -1).transpose(1, 0, 2)
    k = unpack_weight(k_words, k_scales, "e4m3")
    kg = pick(k, idx)
    qq = mxq(f64(qT), 1, "e4m3")
    a = qq.transpose(0, 2, 1) @ kg
    y = np.square(np.maximum(a, 0.0))
    return y

@@ -1,0 +1,90 @@
+from contextlib import ExitStack
+
+import concourse.mybir as mybir
+
+F32 = mybir.dt.float32
+BF16 = mybir.dt.bfloat16
+I32 = mybir.dt.int32
+U32 = mybir.dt.uint32
+U16 = mybir.dt.uint16
+U8 = mybir.dt.uint8
+FP8X4 = mybir.dt.float8_e4m3fn_x4
+ACT = mybir.ActivationFunctionType
+ALU = mybir.AluOpType
+
+P = 128
+PACK = 4
+D, T, N, NQ = 512, 4096, 512, 256
+FLOPS = 2 * NQ * N * D
+VEC_COLS = 80
+CHUNKS = ((0, 0, 256), (0, 256, 512), (1, 0, 256), (1, 256, 384), (1, 384, 512))
+
+
+def tile_attend_neu_relu2_srt_kernel(tc, qT, k_words, k_scales, offs, out):
+    nc = tc.nc
+    with ExitStack() as ctx:
+        pool = ctx.enter_context(tc.tile_pool(name="held", bufs=1))
+        psum = ctx.enter_context(tc.psum_pool(name="psum", bufs=1))
+
+        offsets = pool.tile([P, N // 16], U16, name="offsets")
+        nc.sync.dma_start(offsets[:], offs)
+
+        table_scales = pool.tile([P, T], U8, name="table_scales", align_bytes=64)
+        nc.vector.memset(table_scales[:].bitcast(I32), 0)
+        nc.scalar.dma_start(table_scales[0:P:8, :].bitcast(I32), k_scales[0].bitcast(I32))
+        key_scales = pool.tile([P, N], U8, name="key_scales", align_bytes=64)
+        nc.vector.memset(key_scales[:].bitcast(I32), 0)
+
+        warm_in = pool.tile([P, 8], F32, name="warm_in")
+        warm_out = pool.tile([P, 8], F32, name="warm_out")
+        nc.vector.memset(warm_in[:], 0.0)
+        nc.scalar.activation(warm_out[:], warm_in[:], ACT.Relu)
+
+        table_words = pool.tile([P, T], I32, name="table_words", align_bytes=64)
+        q_raw = pool.tile([P, PACK, NQ], F32, name="q_raw", align_bytes=64)
+        nc.sync.dma_start(table_words[:], k_words[0].rearrange("p n t -> p (n t)").bitcast(I32), max_dma_last_dim=4096)
+        nc.sync.dma_start(q_raw[:], qT[0].rearrange("(p j) c -> p j c", j=PACK))
+
+        picked_scales = pool.tile([P, N], U8, name="picked_scales", align_bytes=64)
+        nc.vector.tensor_copy(picked_scales[:], table_scales[:].indirect(offsets[:]))
+        for quad in range(4):
+            nc.scalar.dma_start(
+                key_scales[32 * quad : 32 * quad + 4, :].bitcast(I32),
+                picked_scales[32 * quad : 32 * quad + 32 : 8, :].bitcast(I32),
+            )
+
+        key_words = pool.tile([P, N], U32, name="key_words", align_bytes=64)
+        nc.vector.tensor_copy(key_words[:], table_words[:].bitcast(U32).indirect(offsets[:]))
+
+        grouped = [pool.tile([P, P, PACK], BF16, name=f"grouped{h}", align_bytes=64) for h in range(2)]
+        for h in range(2):
+            for lo, hi, copy in ((0, VEC_COLS, nc.vector.tensor_copy), (VEC_COLS, P, nc.scalar.copy)):
+                copy(
+                    grouped[h][:, lo:hi, :].rearrange("p (c i) t -> p c t i", i=4),
+                    q_raw[:, :, h * P + lo : h * P + hi].rearrange("p t (c i) -> p c t i", i=4),
+                )
+        q_words = [pool.tile([P, P], U32, name=f"q_words{h}", align_bytes=64) for h in range(2)]
+        q_scales = [pool.tile([P, P], U8, name=f"q_scales{h}", align_bytes=64) for h in range(2)]
+        for h in range(2):
+            nc.vector.quantize_mx(
+                out=q_words[h][:].bitcast(FP8X4),
+                scales=q_scales[h][:],
+                in_=grouped[h][:].rearrange("p c t -> p (c t)"),
+            )
+
+        for c, (h, lo, hi) in enumerate(CHUNKS):
+            acc = psum.tile([P, hi - lo], F32, name=f"acc{c}")
+            nc.tensor.matmul_mx(
+                out=acc[:],
+                lhsT=q_words[h][:].bitcast(FP8X4),
+                lhsT_scale=q_scales[h][:],
+                rhs=key_words[:, lo:hi].bitcast(FP8X4),
+                rhs_scale=key_scales[:, lo:hi],
+                start=True,
+                stop=True,
+            )
+            rect = pool.tile([P, hi - lo], F32, name=f"rect{c}")
+            nc.scalar.activation(rect[:], acc[:], ACT.Relu)
+            squared = pool.tile([P, hi - lo], F32, name=f"squared{c}")
+            nc.vector.tensor_tensor(squared[:], rect[:], rect[:], ALU.mult)
+            nc.sync.dma_start(out[0, h * P : (h + 1) * P, lo:hi], squared[:])

@@ -16,8 +16,8 @@ P = 128
 PACK = 4
 D, T, N, NQ = 512, 4096, 512, 256
 FLOPS = 2 * NQ * N * D
-VEC_COLS = 80
-CHUNKS = ((0, 0, 256), (0, 256, 512), (1, 0, 256), (1, 256, 384), (1, 384, 512))
+VEC_COLS = 88
+CHUNKS = ((0, 0, 128, (128,)), (0, 128, 256, (128,)), (0, 256, 512, (128, 128)), (1, 0, 256, (128, 128)), (1, 256, 384, (128,)), (1, 384, 512, (128,)))
 
 
 def tile_attend_neu_relu2_srt_kernel(tc, qT, k_words, k_scales, offs, out):
@@ -26,19 +26,13 @@ def tile_attend_neu_relu2_srt_kernel(tc, qT, k_words, k_scales, offs, out):
         pool = ctx.enter_context(tc.tile_pool(name="held", bufs=1))
         psum = ctx.enter_context(tc.psum_pool(name="psum", bufs=1))
 
+        table_scales = pool.tile([P, T], U8, name="table_scales", align_bytes=64)
+        nc.sync.dma_start(table_scales[112:P, :].bitcast(I32), k_scales[0].bitcast(I32))
         offsets = pool.tile([P, N // 16], U16, name="offsets")
         nc.sync.dma_start(offsets[:], offs)
-
-        table_scales = pool.tile([P, T], U8, name="table_scales", align_bytes=64)
-        nc.vector.memset(table_scales[:].bitcast(I32), 0)
-        nc.scalar.dma_start(table_scales[0:P:8, :].bitcast(I32), k_scales[0].bitcast(I32))
+        nc.vector.memset(table_scales[0:112, :].bitcast(I32), 0)
         key_scales = pool.tile([P, N], U8, name="key_scales", align_bytes=64)
         nc.vector.memset(key_scales[:].bitcast(I32), 0)
-
-        warm_in = pool.tile([P, 8], F32, name="warm_in")
-        warm_out = pool.tile([P, 8], F32, name="warm_out")
-        nc.vector.memset(warm_in[:], 0.0)
-        nc.scalar.activation(warm_out[:], warm_in[:], ACT.Relu)
 
         table_words = pool.tile([P, T], I32, name="table_words", align_bytes=64)
         q_raw = pool.tile([P, PACK, NQ], F32, name="q_raw", align_bytes=64)
@@ -50,7 +44,7 @@ def tile_attend_neu_relu2_srt_kernel(tc, qT, k_words, k_scales, offs, out):
         for quad in range(4):
             nc.scalar.dma_start(
                 key_scales[32 * quad : 32 * quad + 4, :].bitcast(I32),
-                picked_scales[32 * quad : 32 * quad + 32 : 8, :].bitcast(I32),
+                picked_scales[112 + 4 * quad : 116 + 4 * quad, :].bitcast(I32),
             )
 
         key_words = pool.tile([P, N], U32, name="key_words", align_bytes=64)
@@ -72,19 +66,22 @@ def tile_attend_neu_relu2_srt_kernel(tc, qT, k_words, k_scales, offs, out):
                 in_=grouped[h][:].rearrange("p c t -> p (c t)"),
             )
 
-        for c, (h, lo, hi) in enumerate(CHUNKS):
-            acc = psum.tile([P, hi - lo], F32, name=f"acc{c}")
-            nc.tensor.matmul_mx(
-                out=acc[:],
-                lhsT=q_words[h][:].bitcast(FP8X4),
-                lhsT_scale=q_scales[h][:],
-                rhs=key_words[:, lo:hi].bitcast(FP8X4),
-                rhs_scale=key_scales[:, lo:hi],
-                start=True,
-                stop=True,
-            )
-            rect = pool.tile([P, hi - lo], F32, name=f"rect{c}")
-            nc.scalar.activation(rect[:], acc[:], ACT.Relu)
-            squared = pool.tile([P, hi - lo], F32, name=f"squared{c}")
-            nc.vector.tensor_tensor(squared[:], rect[:], rect[:], ALU.mult)
+        for h, lo, hi, widths in CHUNKS:
+            squared = pool.tile([P, hi - lo], F32, name=f"squared{h}_{lo}")
+            at = lo
+            for width in widths:
+                acc = psum.tile([P, width], F32, name=f"acc{h}_{at}")
+                nc.tensor.matmul_mx(
+                    out=acc[:],
+                    lhsT=q_words[h][:].bitcast(FP8X4),
+                    lhsT_scale=q_scales[h][:],
+                    rhs=key_words[:, at : at + width].bitcast(FP8X4),
+                    rhs_scale=key_scales[:, at : at + width],
+                    start=True,
+                    stop=True,
+                )
+                rect = pool.tile([P, width], F32, name=f"rect{h}_{at}")
+                nc.scalar.activation(rect[:], acc[:], ACT.Relu)
+                nc.vector.tensor_tensor(squared[:, at - lo : at - lo + width], rect[:], rect[:], ALU.mult)
+                at += width
             nc.sync.dma_start(out[0, h * P : (h + 1) * P, lo:hi], squared[:])

@@ -16,7 +16,7 @@ P = 128
 PACK = 4
 D, T, N, NQ = 512, 4096, 512, 256
 FLOPS = 2 * NQ * N * D
-VEC_COLS = 88
+VEC_COLS = 64
 CHUNKS = ((0, 0, 128, (128,)), (0, 128, 256, (128,)), (0, 256, 512, (128, 128)), (1, 0, 256, (128, 128)), (1, 256, 384, (128,)), (1, 384, 512, (128,)))
 
 
@@ -36,7 +36,7 @@ def tile_attend_neu_relu2_srt_kernel(tc, qT, k_words, k_scales, offs, out):
 
         table_words = pool.tile([P, T], I32, name="table_words", align_bytes=64)
         q_raw = pool.tile([P, PACK, NQ], F32, name="q_raw", align_bytes=64)
-        nc.sync.dma_start(table_words[:], k_words[0].rearrange("p n t -> p (n t)").bitcast(I32), max_dma_last_dim=4096)
+        nc.sync.dma_start(table_words[:], k_words[0].rearrange("p n t -> p (n t)").bitcast(I32))
         nc.sync.dma_start(q_raw[:], qT[0].rearrange("(p j) c -> p j c", j=PACK))
 
         picked_scales = pool.tile([P, N], U8, name="picked_scales", align_bytes=64)

@@ -16,7 +16,7 @@ P = 128
 PACK = 4
 D, T, N, NQ = 512, 4096, 512, 256
 FLOPS = 2 * NQ * N * D
-VEC_COLS = 64
+HEAD_COLS = 1024
 CHUNKS = ((0, 0, 128, (128,)), (0, 128, 256, (128,)), (0, 256, 512, (128, 128)), (1, 0, 256, (128, 128)), (1, 256, 384, (128,)), (1, 384, 512, (128,)))
 
 
@@ -26,25 +26,30 @@ def tile_attend_neu_relu2_srt_kernel(tc, qT, k_words, k_scales, offs, out):
         pool = ctx.enter_context(tc.tile_pool(name="held", bufs=1))
         psum = ctx.enter_context(tc.psum_pool(name="psum", bufs=1))
 
-        table_scales = pool.tile([P, T], U8, name="table_scales", align_bytes=64)
-        nc.sync.dma_start(table_scales[112:P, :].bitcast(I32), k_scales[0].bitcast(I32))
         offsets = pool.tile([P, N // 16], U16, name="offsets")
         nc.sync.dma_start(offsets[:], offs)
-        nc.vector.memset(table_scales[0:112, :].bitcast(I32), 0)
+        table_scales = pool.tile([P, T], U8, name="table_scales", align_bytes=64)
+        nc.vector.memset(table_scales[:].bitcast(I32), 0)
         key_scales = pool.tile([P, N], U8, name="key_scales", align_bytes=64)
         nc.vector.memset(key_scales[:].bitcast(I32), 0)
 
         table_words = pool.tile([P, T], I32, name="table_words", align_bytes=64)
-        q_raw = pool.tile([P, PACK, NQ], F32, name="q_raw", align_bytes=64)
-        nc.sync.dma_start(table_words[:], k_words[0].rearrange("p n t -> p (n t)").bitcast(I32))
-        nc.sync.dma_start(q_raw[:], qT[0].rearrange("(p j) c -> p j c", j=PACK))
+        words_hbm = k_words[0].rearrange("p n t -> p (n t)").bitcast(I32)
+        nc.sync.dma_start(table_words[:, :HEAD_COLS], words_hbm[:, :HEAD_COLS])
+        nc.sync.dma_start(table_scales[32:96:4, :].bitcast(I32), k_scales[0].bitcast(I32))
+        nc.sync.dma_start(table_words[:, HEAD_COLS:], words_hbm[:, HEAD_COLS:])
+
+        q_hbm = qT[0].rearrange("(p j) c -> p j c", j=PACK)
+        q_raw = [pool.tile([P, PACK, P], F32, name=f"q_raw{h}", align_bytes=64) for h in range(2)]
+        for h in range(2):
+            nc.sync.dma_start(q_raw[h][:], q_hbm[:, :, h * P : (h + 1) * P])
 
         picked_scales = pool.tile([P, N], U8, name="picked_scales", align_bytes=64)
         nc.vector.tensor_copy(picked_scales[:], table_scales[:].indirect(offsets[:]))
         for quad in range(4):
-            nc.scalar.dma_start(
+            nc.sync.dma_start(
                 key_scales[32 * quad : 32 * quad + 4, :].bitcast(I32),
-                picked_scales[112 + 4 * quad : 116 + 4 * quad, :].bitcast(I32),
+                picked_scales[32 + 16 * quad : 48 + 16 * quad : 4, :].bitcast(I32),
             )
 
         key_words = pool.tile([P, N], U32, name="key_words", align_bytes=64)
@@ -52,11 +57,10 @@ def tile_attend_neu_relu2_srt_kernel(tc, qT, k_words, k_scales, offs, out):
 
         grouped = [pool.tile([P, P, PACK], BF16, name=f"grouped{h}", align_bytes=64) for h in range(2)]
         for h in range(2):
-            for lo, hi, copy in ((0, VEC_COLS, nc.vector.tensor_copy), (VEC_COLS, P, nc.scalar.copy)):
-                copy(
-                    grouped[h][:, lo:hi, :].rearrange("p (c i) t -> p c t i", i=4),
-                    q_raw[:, :, h * P + lo : h * P + hi].rearrange("p t (c i) -> p c t i", i=4),
-                )
+            nc.scalar.copy(
+                grouped[h][:].rearrange("p (c i) t -> p c t i", i=4),
+                q_raw[h][:].rearrange("p t (c i) -> p c t i", i=4),
+            )
         q_words = [pool.tile([P, P], U32, name=f"q_words{h}", align_bytes=64) for h in range(2)]
         q_scales = [pool.tile([P, P], U8, name=f"q_scales{h}", align_bytes=64) for h in range(2)]
         for h in range(2):

@@ -17,6 +17,7 @@ PACK = 4
 D, T, N, NQ = 512, 4096, 512, 256
 FLOPS = 2 * NQ * N * D
 HEAD_COLS = 1024
+VEC_COLS = 64
 CHUNKS = ((0, 0, 128, (128,)), (0, 128, 256, (128,)), (0, 256, 512, (128, 128)), (1, 0, 256, (128, 128)), (1, 256, 384, (128,)), (1, 384, 512, (128,)))
 
 
@@ -26,8 +27,6 @@ def tile_attend_neu_relu2_srt_kernel(tc, qT, k_words, k_scales, offs, out):
         pool = ctx.enter_context(tc.tile_pool(name="held", bufs=1))
         psum = ctx.enter_context(tc.psum_pool(name="psum", bufs=1))
 
-        offsets = pool.tile([P, N // 16], U16, name="offsets")
-        nc.sync.dma_start(offsets[:], offs)
         table_scales = pool.tile([P, T], U8, name="table_scales", align_bytes=64)
         nc.vector.memset(table_scales[:].bitcast(I32), 0)
         key_scales = pool.tile([P, N], U8, name="key_scales", align_bytes=64)
@@ -36,13 +35,13 @@ def tile_attend_neu_relu2_srt_kernel(tc, qT, k_words, k_scales, offs, out):
         table_words = pool.tile([P, T], I32, name="table_words", align_bytes=64)
         words_hbm = k_words[0].rearrange("p n t -> p (n t)").bitcast(I32)
         nc.sync.dma_start(table_words[:, :HEAD_COLS], words_hbm[:, :HEAD_COLS])
+        offsets = pool.tile([P, N // 16], U16, name="offsets")
+        nc.sync.dma_start(offsets[:], offs)
         nc.sync.dma_start(table_scales[32:96:4, :].bitcast(I32), k_scales[0].bitcast(I32))
         nc.sync.dma_start(table_words[:, HEAD_COLS:], words_hbm[:, HEAD_COLS:])
 
-        q_hbm = qT[0].rearrange("(p j) c -> p j c", j=PACK)
-        q_raw = [pool.tile([P, PACK, P], F32, name=f"q_raw{h}", align_bytes=64) for h in range(2)]
-        for h in range(2):
-            nc.sync.dma_start(q_raw[h][:], q_hbm[:, :, h * P : (h + 1) * P])
+        q_raw = pool.tile([P, PACK, NQ], F32, name="q_raw", align_bytes=64)
+        nc.sync.dma_start(q_raw[:], qT[0].rearrange("(p j) c -> p j c", j=PACK))
 
         picked_scales = pool.tile([P, N], U8, name="picked_scales", align_bytes=64)
         nc.vector.tensor_copy(picked_scales[:], table_scales[:].indirect(offsets[:]))
@@ -57,10 +56,11 @@ def tile_attend_neu_relu2_srt_kernel(tc, qT, k_words, k_scales, offs, out):
 
         grouped = [pool.tile([P, P, PACK], BF16, name=f"grouped{h}", align_bytes=64) for h in range(2)]
         for h in range(2):
-            nc.scalar.copy(
-                grouped[h][:].rearrange("p (c i) t -> p c t i", i=4),
-                q_raw[h][:].rearrange("p t (c i) -> p c t i", i=4),
-            )
+            for lo, hi, copy in ((0, VEC_COLS, nc.vector.tensor_copy), (VEC_COLS, P, nc.scalar.copy)):
+                copy(
+                    grouped[h][:, lo:hi, :].rearrange("p (c i) t -> p c t i", i=4),
+                    q_raw[:, :, h * P + lo : h * P + hi].rearrange("p t (c i) -> p c t i", i=4),
+                )
         q_words = [pool.tile([P, P], U32, name=f"q_words{h}", align_bytes=64) for h in range(2)]
         q_scales = [pool.tile([P, P], U8, name=f"q_scales{h}", align_bytes=64) for h in range(2)]
         for h in range(2):

@@ -18,7 +18,7 @@ D, T, N, NQ = 512, 4096, 512, 256
 FLOPS = 2 * NQ * N * D
 HEAD_COLS = 1024
 VEC_COLS = 64
-CHUNKS = ((0, 0, 128, (128,)), (0, 128, 256, (128,)), (0, 256, 512, (128, 128)), (1, 0, 256, (128, 128)), (1, 256, 384, (128,)), (1, 384, 512, (128,)))
+CHUNKS = ((0, 0, 128, (128,)), (0, 128, 256, (128,)), (0, 256, 512, (128, 128)), (1, 0, 256, (128, 128)), (1, 256, 512, (128, 128)))
 
 
 def tile_attend_neu_relu2_srt_kernel(tc, qT, k_words, k_scales, offs, out):

@@ -46,10 +46,13 @@ def tile_attend_neu_relu2_srt_kernel(tc, qT, k_words, k_scales, offs, out):
         picked_scales = pool.tile([P, N], U8, name="picked_scales", align_bytes=64)
         nc.vector.tensor_copy(picked_scales[:], table_scales[:].indirect(offsets[:]))
         for quad in range(4):
-            nc.sync.dma_start(
-                key_scales[32 * quad : 32 * quad + 4, :].bitcast(I32),
-                picked_scales[32 + 16 * quad : 48 + 16 * quad : 4, :].bitcast(I32),
-            )
+            rows = 2 if quad >= 2 else 4
+            for row in range(0, 4, rows):
+                first = 32 + 4 * (4 * quad + row)
+                nc.sync.dma_start(
+                    key_scales[32 * quad + row : 32 * quad + row + rows, :].bitcast(I32),
+                    picked_scales[first : first + 4 * rows : 4, :].bitcast(I32),
+                )
 
         key_words = pool.tile([P, N], U32, name="key_words", align_bytes=64)
         nc.vector.tensor_copy(key_words[:], table_words[:].bitcast(U32).indirect(offsets[:]))

@@ -27,12 +27,12 @@ def tile_attend_neu_relu2_srt_kernel(tc, qT, k_words, k_scales, offs, out):
         pool = ctx.enter_context(tc.tile_pool(name="held", bufs=1))
         psum = ctx.enter_context(tc.psum_pool(name="psum", bufs=1))
 
-        table_scales = pool.tile([P, T], U8, name="table_scales", align_bytes=64)
+        table_scales = pool.tile([P, T], U8, name="table_scales", align_bytes=256)
         nc.vector.memset(table_scales[:].bitcast(I32), 0)
-        key_scales = pool.tile([P, N], U8, name="key_scales", align_bytes=64)
+        key_scales = pool.tile([P, N], U8, name="key_scales", align_bytes=256)
         nc.vector.memset(key_scales[:].bitcast(I32), 0)
 
-        table_words = pool.tile([P, T], I32, name="table_words", align_bytes=64)
+        table_words = pool.tile([P, T], I32, name="table_words", align_bytes=256)
         words_hbm = k_words[0].rearrange("p n t -> p (n t)").bitcast(I32)
         nc.sync.dma_start(table_words[:, :HEAD_COLS], words_hbm[:, :HEAD_COLS])
         offsets = pool.tile([P, N // 16], U16, name="offsets")
@@ -40,10 +40,10 @@ def tile_attend_neu_relu2_srt_kernel(tc, qT, k_words, k_scales, offs, out):
         nc.sync.dma_start(table_scales[32:96:4, :].bitcast(I32), k_scales[0].bitcast(I32))
         nc.sync.dma_start(table_words[:, HEAD_COLS:], words_hbm[:, HEAD_COLS:])
 
-        q_raw = pool.tile([P, PACK, NQ], F32, name="q_raw", align_bytes=64)
+        q_raw = pool.tile([P, PACK, NQ], F32, name="q_raw", align_bytes=256)
         nc.sync.dma_start(q_raw[:], qT[0].rearrange("(p j) c -> p j c", j=PACK))
 
-        picked_scales = pool.tile([P, N], U8, name="picked_scales", align_bytes=64)
+        picked_scales = pool.tile([P, N], U8, name="picked_scales", align_bytes=256)
         nc.vector.tensor_copy(picked_scales[:], table_scales[:].indirect(offsets[:]))
         for quad in range(4):
             rows = 2 if quad >= 2 else 4
@@ -54,18 +54,18 @@ def tile_attend_neu_relu2_srt_kernel(tc, qT, k_words, k_scales, offs, out):
                     picked_scales[first : first + 4 * rows : 4, :].bitcast(I32),
                 )
 
-        key_words = pool.tile([P, N], U32, name="key_words", align_bytes=64)
+        key_words = pool.tile([P, N], U32, name="key_words", align_bytes=256)
         nc.vector.tensor_copy(key_words[:], table_words[:].bitcast(U32).indirect(offsets[:]))
 
-        grouped = [pool.tile([P, P, PACK], BF16, name=f"grouped{h}", align_bytes=64) for h in range(2)]
+        grouped = [pool.tile([P, P, PACK], BF16, name=f"grouped{h}", align_bytes=256) for h in range(2)]
         for h in range(2):
             for lo, hi, copy in ((0, VEC_COLS, nc.vector.tensor_copy), (VEC_COLS, P, nc.scalar.copy)):
                 copy(
                     grouped[h][:, lo:hi, :].rearrange("p (c i) t -> p c t i", i=4),
                     q_raw[:, :, h * P + lo : h * P + hi].rearrange("p t (c i) -> p c t i", i=4),
                 )
-        q_words = [pool.tile([P, P], U32, name=f"q_words{h}", align_bytes=64) for h in range(2)]
-        q_scales = [pool.tile([P, P], U8, name=f"q_scales{h}", align_bytes=64) for h in range(2)]
+        q_words = [pool.tile([P, P], U32, name=f"q_words{h}", align_bytes=256) for h in range(2)]
+        q_scales = [pool.tile([P, P], U8, name=f"q_scales{h}", align_bytes=256) for h in range(2)]
         for h in range(2):
             nc.vector.quantize_mx(
                 out=q_words[h][:].bitcast(FP8X4),

@@ -17,7 +17,7 @@ PACK = 4
 D, T, N, NQ = 512, 4096, 512, 256
 FLOPS = 2 * NQ * N * D
 HEAD_COLS = 1024
-VEC_COLS = 64
+VEC_COLS = (0, 0)
 CHUNKS = ((0, 0, 128, (128,)), (0, 128, 256, (128,)), (0, 256, 512, (128, 128)), (1, 0, 256, (128, 128)), (1, 256, 512, (128, 128)))
 
 
@@ -38,15 +38,16 @@ def tile_attend_neu_relu2_srt_kernel(tc, qT, k_words, k_scales, offs, out):
         offsets = pool.tile([P, N // 16], U16, name="offsets")
         nc.sync.dma_start(offsets[:], offs)
         nc.sync.dma_start(table_scales[32:96:4, :].bitcast(I32), k_scales[0].bitcast(I32))
+        q_hbm = qT[0].rearrange("(p j) c -> p j c", j=PACK)
+        q_raw = [pool.tile([P, PACK, P], F32, name=f"q_raw{h}", align_bytes=256) for h in range(2)]
+        nc.sync.dma_start(q_raw[0][:], q_hbm[:, :, :P])
         nc.sync.dma_start(table_words[:, HEAD_COLS:], words_hbm[:, HEAD_COLS:])
-
-        q_raw = pool.tile([P, PACK, NQ], F32, name="q_raw", align_bytes=256)
-        nc.sync.dma_start(q_raw[:], qT[0].rearrange("(p j) c -> p j c", j=PACK))
+        nc.sync.dma_start(q_raw[1][:], q_hbm[:, :, P:])
 
         picked_scales = pool.tile([P, N], U8, name="picked_scales", align_bytes=256)
         nc.vector.tensor_copy(picked_scales[:], table_scales[:].indirect(offsets[:]))
         for quad in range(4):
-            rows = 2 if quad >= 2 else 4
+            rows = 4
             for row in range(0, 4, rows):
                 first = 32 + 4 * (4 * quad + row)
                 nc.sync.dma_start(
@@ -59,11 +60,12 @@ def tile_attend_neu_relu2_srt_kernel(tc, qT, k_words, k_scales, offs, out):
 
         grouped = [pool.tile([P, P, PACK], BF16, name=f"grouped{h}", align_bytes=256) for h in range(2)]
         for h in range(2):
-            for lo, hi, copy in ((0, VEC_COLS, nc.vector.tensor_copy), (VEC_COLS, P, nc.scalar.copy)):
-                copy(
-                    grouped[h][:, lo:hi, :].rearrange("p (c i) t -> p c t i", i=4),
-                    q_raw[:, :, h * P + lo : h * P + hi].rearrange("p t (c i) -> p c t i", i=4),
-                )
+            for lo, hi, copy in ((0, VEC_COLS[h], nc.vector.tensor_copy), (VEC_COLS[h], P, nc.scalar.copy)):
+                if hi > lo:
+                    copy(
+                        grouped[h][:, lo:hi, :].rearrange("p (c i) t -> p c t i", i=4),
+                        q_raw[h][:, :, lo:hi].rearrange("p t (c i) -> p c t i", i=4),
+                    )
         q_words = [pool.tile([P, P], U32, name=f"q_words{h}", align_bytes=256) for h in range(2)]
         q_scales = [pool.tile([P, P], U8, name=f"q_scales{h}", align_bytes=256) for h in range(2)]
         for h in range(2):
@@ -74,7 +76,7 @@ def tile_attend_neu_relu2_srt_kernel(tc, qT, k_words, k_scales, offs, out):
             )
 
         for h, lo, hi, widths in CHUNKS:
-            squared = pool.tile([P, hi - lo], F32, name=f"squared{h}_{lo}")
+            squared = pool.tile([P, hi - lo], F32, name=f"squared{h}_{lo}", align_bytes=256)
             at = lo
             for width in widths:
                 acc = psum.tile([P, width], F32, name=f"acc{h}_{at}")

@@ -17,7 +17,7 @@ PACK = 4
 D, T, N, NQ = 512, 4096, 512, 256
 FLOPS = 2 * NQ * N * D
 HEAD_COLS = 1024
-VEC_COLS = (0, 0)
+VEC_COLS = (128, 0)
 CHUNKS = ((0, 0, 128, (128,)), (0, 128, 256, (128,)), (0, 256, 512, (128, 128)), (1, 0, 256, (128, 128)), (1, 256, 512, (128, 128)))
 
 
@@ -34,7 +34,8 @@ def tile_attend_neu_relu2_srt_kernel(tc, qT, k_words, k_scales, offs, out):
 
         table_words = pool.tile([P, T], I32, name="table_words", align_bytes=256)
         words_hbm = k_words[0].rearrange("p n t -> p (n t)").bitcast(I32)
-        nc.sync.dma_start(table_words[:, :HEAD_COLS], words_hbm[:, :HEAD_COLS])
+        head_words = pool.tile([P, HEAD_COLS], I32, name="head_words", align_bytes=256)
+        nc.sync.dma_start(head_words[:], words_hbm[:, :HEAD_COLS])
         offsets = pool.tile([P, N // 16], U16, name="offsets")
         nc.sync.dma_start(offsets[:], offs)
         nc.sync.dma_start(table_scales[32:96:4, :].bitcast(I32), k_scales[0].bitcast(I32))
@@ -44,6 +45,7 @@ def tile_attend_neu_relu2_srt_kernel(tc, qT, k_words, k_scales, offs, out):
         nc.sync.dma_start(table_words[:, HEAD_COLS:], words_hbm[:, HEAD_COLS:])
         nc.sync.dma_start(q_raw[1][:], q_hbm[:, :, P:])
 
+        nc.vector.tensor_copy(table_words[:, :HEAD_COLS], head_words[:])
         picked_scales = pool.tile([P, N], U8, name="picked_scales", align_bytes=256)
         nc.vector.tensor_copy(picked_scales[:], table_scales[:].indirect(offsets[:]))
         for quad in range(4):

@@ -16,9 +16,15 @@ P = 128
 PACK = 4
 D, T, N, NQ = 512, 4096, 512, 256
 FLOPS = 2 * NQ * N * D
+HALVES = NQ // P
+QUADS, QUAD = 4, 32
+QUAD_ROWS = 4
+SPREAD_FIRST, SPREAD_STEP = 32, 4
 HEAD_COLS = 1024
-VEC_COLS = (128, 0)
-CHUNKS = ((0, 0, 128, (128,)), (0, 128, 256, (128,)), (0, 256, 512, (128, 128)), (1, 0, 256, (128, 128)), (1, 256, 512, (128, 128)))
+RUN = 4
+WIDTH = 128
+Q_PIECES = ((0, 0, 128), (1, 0, 64), (1, 64, 128))
+STORES = ((0, 0, 128), (0, 128, 256), (0, 256, 512), (1, 0, 256), (1, 256, 512))
 
 
 def tile_attend_neu_relu2_srt_kernel(tc, qT, k_words, k_scales, offs, out):
@@ -36,63 +42,59 @@ def tile_attend_neu_relu2_srt_kernel(tc, qT, k_words, k_scales, offs, out):
         words_hbm = k_words[0].rearrange("p n t -> p (n t)").bitcast(I32)
         head_words = pool.tile([P, HEAD_COLS], I32, name="head_words", align_bytes=256)
         nc.sync.dma_start(head_words[:], words_hbm[:, :HEAD_COLS])
+        q_hbm = qT[0].rearrange("(p j) c -> p j c", j=PACK)
+        q_raw = [pool.tile([P, PACK, P], F32, name=f"q_raw{h}", align_bytes=256) for h in range(HALVES)]
+        nc.sync.dma_start(q_raw[0][:], q_hbm[:, :, :P])
         offsets = pool.tile([P, N // 16], U16, name="offsets")
         nc.sync.dma_start(offsets[:], offs)
-        nc.sync.dma_start(table_scales[32:96:4, :].bitcast(I32), k_scales[0].bitcast(I32))
-        q_hbm = qT[0].rearrange("(p j) c -> p j c", j=PACK)
-        q_raw = [pool.tile([P, PACK, P], F32, name=f"q_raw{h}", align_bytes=256) for h in range(2)]
-        nc.sync.dma_start(q_raw[0][:], q_hbm[:, :, :P])
+        spread_end = SPREAD_FIRST + SPREAD_STEP * QUADS * QUAD_ROWS
+        nc.sync.dma_start(table_scales[SPREAD_FIRST:spread_end:SPREAD_STEP, :].bitcast(I32), k_scales[0].bitcast(I32))
         nc.sync.dma_start(table_words[:, HEAD_COLS:], words_hbm[:, HEAD_COLS:])
         nc.sync.dma_start(q_raw[1][:], q_hbm[:, :, P:])
 
         nc.vector.tensor_copy(table_words[:, :HEAD_COLS], head_words[:])
+
         picked_scales = pool.tile([P, N], U8, name="picked_scales", align_bytes=256)
         nc.vector.tensor_copy(picked_scales[:], table_scales[:].indirect(offsets[:]))
-        for quad in range(4):
-            rows = 4
-            for row in range(0, 4, rows):
-                first = 32 + 4 * (4 * quad + row)
-                nc.sync.dma_start(
-                    key_scales[32 * quad + row : 32 * quad + row + rows, :].bitcast(I32),
-                    picked_scales[first : first + 4 * rows : 4, :].bitcast(I32),
-                )
+        for quad in range(QUADS):
+            first = SPREAD_FIRST + SPREAD_STEP * QUAD_ROWS * quad
+            nc.sync.dma_start(
+                key_scales[QUAD * quad : QUAD * quad + QUAD_ROWS, :].bitcast(I32),
+                picked_scales[first : first + SPREAD_STEP * QUAD_ROWS : SPREAD_STEP, :].bitcast(I32),
+            )
 
         key_words = pool.tile([P, N], U32, name="key_words", align_bytes=256)
         nc.vector.tensor_copy(key_words[:], table_words[:].bitcast(U32).indirect(offsets[:]))
 
-        grouped = [pool.tile([P, P, PACK], BF16, name=f"grouped{h}", align_bytes=256) for h in range(2)]
-        for h in range(2):
-            for lo, hi, copy in ((0, VEC_COLS[h], nc.vector.tensor_copy), (VEC_COLS[h], P, nc.scalar.copy)):
-                if hi > lo:
-                    copy(
-                        grouped[h][:, lo:hi, :].rearrange("p (c i) t -> p c t i", i=4),
-                        q_raw[h][:, :, lo:hi].rearrange("p t (c i) -> p c t i", i=4),
-                    )
-        q_words = [pool.tile([P, P], U32, name=f"q_words{h}", align_bytes=256) for h in range(2)]
-        q_scales = [pool.tile([P, P], U8, name=f"q_scales{h}", align_bytes=256) for h in range(2)]
-        for h in range(2):
+        grouped = [pool.tile([P, P, PACK], BF16, name=f"grouped{h}", align_bytes=256) for h in range(HALVES)]
+        q_words = [pool.tile([P, P], U32, name=f"q_words{h}", align_bytes=256) for h in range(HALVES)]
+        q_scales = [pool.tile([P, P], U8, name=f"q_scales{h}", align_bytes=256) for h in range(HALVES)]
+        rounding_copy = (nc.vector.tensor_copy, nc.scalar.copy)
+        for h, lo, hi in Q_PIECES:
+            rounding_copy[h](
+                grouped[h][:, lo:hi, :].rearrange("p (c i) j -> p c j i", i=RUN),
+                q_raw[h][:, :, lo:hi].rearrange("p j (c i) -> p c j i", i=RUN),
+            )
             nc.vector.quantize_mx(
-                out=q_words[h][:].bitcast(FP8X4),
-                scales=q_scales[h][:],
-                in_=grouped[h][:].rearrange("p c t -> p (c t)"),
+                out=q_words[h][:, lo:hi].bitcast(FP8X4),
+                scales=q_scales[h][:, lo:hi],
+                in_=grouped[h][:, lo:hi, :].rearrange("p c j -> p (c j)"),
             )
 
-        for h, lo, hi, widths in CHUNKS:
+        for h, lo, hi in STORES:
             squared = pool.tile([P, hi - lo], F32, name=f"squared{h}_{lo}", align_bytes=256)
-            at = lo
-            for width in widths:
-                acc = psum.tile([P, width], F32, name=f"acc{h}_{at}")
+            for at in range(lo, hi, WIDTH):
+                acc = psum.tile([P, WIDTH], F32, name=f"acc{h}_{at}")
                 nc.tensor.matmul_mx(
                     out=acc[:],
                     lhsT=q_words[h][:].bitcast(FP8X4),
                     lhsT_scale=q_scales[h][:],
-                    rhs=key_words[:, at : at + width].bitcast(FP8X4),
-                    rhs_scale=key_scales[:, at : at + width],
+                    rhs=key_words[:, at : at + WIDTH].bitcast(FP8X4),
+                    rhs_scale=key_scales[:, at : at + WIDTH],
                     start=True,
                     stop=True,
                 )
-                rect = pool.tile([P, width], F32, name=f"rect{h}_{at}")
+                rect = pool.tile([P, WIDTH], F32, name=f"rect{h}_{at}")
                 nc.scalar.activation(rect[:], acc[:], ACT.Relu)
-                nc.vector.tensor_tensor(squared[:, at - lo : at - lo + width], rect[:], rect[:], ALU.mult)
-                at += width
+                nc.vector.tensor_tensor(squared[:, at - lo : at - lo + WIDTH], rect[:], rect[:], ALU.mult)
             nc.sync.dma_start(out[0, h * P : (h + 1) * P, lo:hi], squared[:])

@@ -20,10 +20,11 @@ HALVES = NQ // P
 QUADS, QUAD = 4, 32
 QUAD_ROWS = 4
 SPREAD_FIRST, SPREAD_STEP = 32, 4
-HEAD_COLS = 1024
+HEAD_COLS = 1280
 RUN = 4
 WIDTH = 128
-Q_PIECES = ((0, 0, 128), (1, 0, 64), (1, 64, 128))
+ROUNDING = (("scalar", 0, 64), ("scalar", 64, 80), ("gpsimd", 80, 128))
+Q_PIECE = 64
 STORES = ((0, 0, 128), (0, 128, 256), (0, 256, 512), (1, 0, 256), (1, 256, 512))
 
 
@@ -44,13 +45,13 @@ def tile_attend_neu_relu2_srt_kernel(tc, qT, k_words, k_scales, offs, out):
         nc.sync.dma_start(head_words[:], words_hbm[:, :HEAD_COLS])
         q_hbm = qT[0].rearrange("(p j) c -> p j c", j=PACK)
         q_raw = [pool.tile([P, PACK, P], F32, name=f"q_raw{h}", align_bytes=256) for h in range(HALVES)]
-        nc.sync.dma_start(q_raw[0][:], q_hbm[:, :, :P])
         offsets = pool.tile([P, N // 16], U16, name="offsets")
         nc.sync.dma_start(offsets[:], offs)
         spread_end = SPREAD_FIRST + SPREAD_STEP * QUADS * QUAD_ROWS
         nc.sync.dma_start(table_scales[SPREAD_FIRST:spread_end:SPREAD_STEP, :].bitcast(I32), k_scales[0].bitcast(I32))
         nc.sync.dma_start(table_words[:, HEAD_COLS:], words_hbm[:, HEAD_COLS:])
-        nc.sync.dma_start(q_raw[1][:], q_hbm[:, :, P:])
+        for h in range(HALVES):
+            nc.sync.dma_start(q_raw[h][:], q_hbm[:, :, h * P : (h + 1) * P])
 
         nc.vector.tensor_copy(table_words[:, :HEAD_COLS], head_words[:])
 
@@ -69,17 +70,23 @@ def tile_attend_neu_relu2_srt_kernel(tc, qT, k_words, k_scales, offs, out):
         grouped = [pool.tile([P, P, PACK], BF16, name=f"grouped{h}", align_bytes=256) for h in range(HALVES)]
         q_words = [pool.tile([P, P], U32, name=f"q_words{h}", align_bytes=256) for h in range(HALVES)]
         q_scales = [pool.tile([P, P], U8, name=f"q_scales{h}", align_bytes=256) for h in range(HALVES)]
-        rounding_copy = (nc.vector.tensor_copy, nc.scalar.copy)
-        for h, lo, hi in Q_PIECES:
-            rounding_copy[h](
-                grouped[h][:, lo:hi, :].rearrange("p (c i) j -> p c j i", i=RUN),
-                q_raw[h][:, :, lo:hi].rearrange("p j (c i) -> p c j i", i=RUN),
-            )
-            nc.vector.quantize_mx(
-                out=q_words[h][:, lo:hi].bitcast(FP8X4),
-                scales=q_scales[h][:, lo:hi],
-                in_=grouped[h][:, lo:hi, :].rearrange("p c j -> p (c j)"),
-            )
+        for h in range(HALVES):
+            for engine, lo, hi in ROUNDING:
+                if engine == "scalar":
+                    nc.scalar.copy(
+                        grouped[h][:, lo:hi, :].rearrange("p (c i) j -> p c j i", i=RUN),
+                        q_raw[h][:, :, lo:hi].rearrange("p j (c i) -> p c j i", i=RUN),
+                    )
+                else:
+                    nc.gpsimd.tensor_scalar(
+                        grouped[h][:, lo:hi, :], q_raw[h][:, :, lo:hi].rearrange("p j c -> p c j"), 1.0, 0.0, ALU.mult, ALU.add
+                    )
+            for lo in range(0, P, Q_PIECE):
+                nc.vector.quantize_mx(
+                    out=q_words[h][:, lo : lo + Q_PIECE].bitcast(FP8X4),
+                    scales=q_scales[h][:, lo : lo + Q_PIECE],
+                    in_=grouped[h][:, lo : lo + Q_PIECE, :].rearrange("p c j -> p (c j)"),
+                )
 
         for h, lo, hi in STORES:
             squared = pool.tile([P, hi - lo], F32, name=f"squared{h}_{lo}", align_bytes=256)

@@ -39,6 +39,11 @@ def tile_attend_neu_relu2_srt_kernel(tc, qT, k_words, k_scales, offs, out):
         key_scales = pool.tile([P, N], U8, name="key_scales", align_bytes=256)
         nc.vector.memset(key_scales[:].bitcast(I32), 0)
 
+        warm_in = pool.tile([P, 8], F32, name="warm_in")
+        nc.vector.memset(warm_in[:], 0.0)
+        warm_out = pool.tile([P, 8], F32, name="warm_out")
+        nc.scalar.activation(warm_out[:], warm_in[:], ACT.Relu)
+
         table_words = pool.tile([P, T], I32, name="table_words", align_bytes=256)
         words_hbm = k_words[0].rearrange("p n t -> p (n t)").bitcast(I32)
         head_words = pool.tile([P, HEAD_COLS], I32, name="head_words", align_bytes=256)
@@ -59,7 +64,7 @@ def tile_attend_neu_relu2_srt_kernel(tc, qT, k_words, k_scales, offs, out):
         nc.vector.tensor_copy(picked_scales[:], table_scales[:].indirect(offsets[:]))
         for quad in range(QUADS):
             first = SPREAD_FIRST + SPREAD_STEP * QUAD_ROWS * quad
-            nc.sync.dma_start(
+            nc.scalar.dma_start(
                 key_scales[QUAD * quad : QUAD * quad + QUAD_ROWS, :].bitcast(I32),
                 picked_scales[first : first + SPREAD_STEP * QUAD_ROWS : SPREAD_STEP, :].bitcast(I32),
             )

@@ -23,8 +23,8 @@ SPREAD_FIRST, SPREAD_STEP = 32, 4
 HEAD_COLS = 1280
 RUN = 4
 WIDTH = 128
-ROUNDING = (("scalar", 0, 64), ("scalar", 64, 80), ("gpsimd", 80, 128))
 Q_PIECE = 64
+SCALAR_FIRST = 80
 STORES = ((0, 0, 128), (0, 128, 256), (0, 256, 512), (1, 0, 256), (1, 256, 512))
 
 
@@ -72,26 +72,37 @@ def tile_attend_neu_relu2_srt_kernel(tc, qT, k_words, k_scales, offs, out):
         key_words = pool.tile([P, N], U32, name="key_words", align_bytes=256)
         nc.vector.tensor_copy(key_words[:], table_words[:].bitcast(U32).indirect(offsets[:]))
 
-        grouped = [pool.tile([P, P, PACK], BF16, name=f"grouped{h}", align_bytes=256) for h in range(HALVES)]
+        grouped_first = pool.tile([P, P, PACK], BF16, name="grouped_first", align_bytes=256)
+        grouped_last = pool.tile([P, P, PACK], BF16, name="grouped_last", align_bytes=256)
         q_words = [pool.tile([P, P], U32, name=f"q_words{h}", align_bytes=256) for h in range(HALVES)]
         q_scales = [pool.tile([P, P], U8, name=f"q_scales{h}", align_bytes=256) for h in range(HALVES)]
-        for h in range(HALVES):
-            for engine, lo, hi in ROUNDING:
-                if engine == "scalar":
-                    nc.scalar.copy(
-                        grouped[h][:, lo:hi, :].rearrange("p (c i) j -> p c j i", i=RUN),
-                        q_raw[h][:, :, lo:hi].rearrange("p j (c i) -> p c j i", i=RUN),
-                    )
-                else:
-                    nc.gpsimd.tensor_scalar(
-                        grouped[h][:, lo:hi, :], q_raw[h][:, :, lo:hi].rearrange("p j c -> p c j"), 1.0, 0.0, ALU.mult, ALU.add
-                    )
-            for lo in range(0, P, Q_PIECE):
-                nc.vector.quantize_mx(
-                    out=q_words[h][:, lo : lo + Q_PIECE].bitcast(FP8X4),
-                    scales=q_scales[h][:, lo : lo + Q_PIECE],
-                    in_=grouped[h][:, lo : lo + Q_PIECE, :].rearrange("p c j -> p (c j)"),
-                )
+
+        def round_in_runs(copy, grouped, raw):
+            copy(grouped.rearrange("p (c i) j -> p c j i", i=RUN), raw.rearrange("p j (c i) -> p c j i", i=RUN))
+
+        def quantise(h, lo, grouped):
+            nc.vector.quantize_mx(
+                out=q_words[h][:, lo : lo + Q_PIECE].bitcast(FP8X4),
+                scales=q_scales[h][:, lo : lo + Q_PIECE],
+                in_=grouped.rearrange("p c j -> p (c j)"),
+            )
+
+        round_in_runs(nc.scalar.copy, grouped_first[:, :Q_PIECE, :], q_raw[0][:, :, :Q_PIECE])
+        round_in_runs(nc.scalar.copy, grouped_first[:, Q_PIECE:SCALAR_FIRST, :], q_raw[0][:, :, Q_PIECE:SCALAR_FIRST])
+        nc.gpsimd.tensor_scalar(
+            grouped_first[:, SCALAR_FIRST:, :],
+            q_raw[0][:, :, SCALAR_FIRST:].rearrange("p j c -> p c j"),
+            1.0,
+            0.0,
+            ALU.mult,
+            ALU.add,
+        )
+        quantise(0, 0, grouped_first[:, :Q_PIECE, :])
+        quantise(0, Q_PIECE, grouped_first[:, Q_PIECE:, :])
+        round_in_runs(nc.scalar.copy, grouped_last[:, :Q_PIECE, :], q_raw[1][:, :, :Q_PIECE])
+        round_in_runs(nc.vector.tensor_copy, grouped_last[:, Q_PIECE:, :], q_raw[1][:, :, Q_PIECE:])
+        quantise(1, 0, grouped_last[:, :Q_PIECE, :])
+        quantise(1, Q_PIECE, grouped_last[:, Q_PIECE:, :])
 
         for h, lo, hi in STORES:
             squared = pool.tile([P, hi - lo], F32, name=f"squared{h}_{lo}", align_bytes=256)

@@ -20,12 +20,13 @@ HALVES = NQ // P
 QUADS, QUAD = 4, 32
 QUAD_ROWS = 4
 SPREAD_FIRST, SPREAD_STEP = 32, 4
-HEAD_COLS = 1280
+HEAD_COLS = 768
+PICK = 256
 RUN = 4
 WIDTH = 128
 Q_PIECE = 64
-SCALAR_FIRST = 80
-STORES = ((0, 0, 128), (0, 128, 256), (0, 256, 512), (1, 0, 256), (1, 256, 512))
+SCALAR_SHARE = 80
+STORES = ((0, 0, 256), (0, 256, 512), (1, 0, 128), (1, 128, 384), (1, 384, 512))
 
 
 def tile_attend_neu_relu2_srt_kernel(tc, qT, k_words, k_scales, offs, out):
@@ -39,26 +40,41 @@ def tile_attend_neu_relu2_srt_kernel(tc, qT, k_words, k_scales, offs, out):
         key_scales = pool.tile([P, N], U8, name="key_scales", align_bytes=256)
         nc.vector.memset(key_scales[:].bitcast(I32), 0)
 
-        warm_in = pool.tile([P, 8], F32, name="warm_in")
-        nc.vector.memset(warm_in[:], 0.0)
-        warm_out = pool.tile([P, 8], F32, name="warm_out")
-        nc.scalar.activation(warm_out[:], warm_in[:], ACT.Relu)
-
         table_words = pool.tile([P, T], I32, name="table_words", align_bytes=256)
         words_hbm = k_words[0].rearrange("p n t -> p (n t)").bitcast(I32)
         head_words = pool.tile([P, HEAD_COLS], I32, name="head_words", align_bytes=256)
         nc.sync.dma_start(head_words[:], words_hbm[:, :HEAD_COLS])
         q_hbm = qT[0].rearrange("(p j) c -> p j c", j=PACK)
         q_raw = [pool.tile([P, PACK, P], F32, name=f"q_raw{h}", align_bytes=256) for h in range(HALVES)]
+        nc.sync.dma_start(q_raw[0][:], q_hbm[:, :, :P])
         offsets = pool.tile([P, N // 16], U16, name="offsets")
         nc.sync.dma_start(offsets[:], offs)
         spread_end = SPREAD_FIRST + SPREAD_STEP * QUADS * QUAD_ROWS
         nc.sync.dma_start(table_scales[SPREAD_FIRST:spread_end:SPREAD_STEP, :].bitcast(I32), k_scales[0].bitcast(I32))
         nc.sync.dma_start(table_words[:, HEAD_COLS:], words_hbm[:, HEAD_COLS:])
-        for h in range(HALVES):
-            nc.sync.dma_start(q_raw[h][:], q_hbm[:, :, h * P : (h + 1) * P])
+        nc.sync.dma_start(q_raw[1][:], q_hbm[:, :, P:])
 
         nc.vector.tensor_copy(table_words[:, :HEAD_COLS], head_words[:])
+
+        grouped = [pool.tile([P, P, PACK], BF16, name=f"grouped{h}", align_bytes=256) for h in range(HALVES)]
+        q_words = [pool.tile([P, P], U32, name=f"q_words{h}", align_bytes=256) for h in range(HALVES)]
+        q_scales = [pool.tile([P, P], U8, name=f"q_scales{h}", align_bytes=256) for h in range(HALVES)]
+
+        def round_in_runs(copy, h, lo, hi):
+            copy(
+                grouped[h][:, lo:hi, :].rearrange("p (c i) j -> p c j i", i=RUN),
+                q_raw[h][:, :, lo:hi].rearrange("p j (c i) -> p c j i", i=RUN),
+            )
+
+        def quantise(h, lo):
+            nc.vector.quantize_mx(
+                out=q_words[h][:, lo : lo + Q_PIECE].bitcast(FP8X4),
+                scales=q_scales[h][:, lo : lo + Q_PIECE],
+                in_=grouped[h][:, lo : lo + Q_PIECE, :].rearrange("p c j -> p (c j)"),
+            )
+
+        round_in_runs(nc.scalar.copy, 0, 0, Q_PIECE)
+        round_in_runs(nc.vector.tensor_copy, 0, Q_PIECE, P)
 
         picked_scales = pool.tile([P, N], U8, name="picked_scales", align_bytes=256)
         nc.vector.tensor_copy(picked_scales[:], table_scales[:].indirect(offsets[:]))
@@ -68,41 +84,26 @@ def tile_attend_neu_relu2_srt_kernel(tc, qT, k_words, k_scales, offs, out):
                 key_scales[QUAD * quad : QUAD * quad + QUAD_ROWS, :].bitcast(I32),
                 picked_scales[first : first + SPREAD_STEP * QUAD_ROWS : SPREAD_STEP, :].bitcast(I32),
             )
+        quantise(0, 0)
+        quantise(0, Q_PIECE)
 
-        key_words = pool.tile([P, N], U32, name="key_words", align_bytes=256)
-        nc.vector.tensor_copy(key_words[:], table_words[:].bitcast(U32).indirect(offsets[:]))
+        key_words = [pool.tile([P, PICK], U32, name=f"key_words{g}", align_bytes=256) for g in range(N // PICK)]
+        for g in range(N // PICK):
+            picks = offsets[:, g * PICK // 16 : (g + 1) * PICK // 16]
+            nc.vector.tensor_copy(key_words[g][:], table_words[:].bitcast(U32).indirect(picks))
 
-        grouped_first = pool.tile([P, P, PACK], BF16, name="grouped_first", align_bytes=256)
-        grouped_last = pool.tile([P, P, PACK], BF16, name="grouped_last", align_bytes=256)
-        q_words = [pool.tile([P, P], U32, name=f"q_words{h}", align_bytes=256) for h in range(HALVES)]
-        q_scales = [pool.tile([P, P], U8, name=f"q_scales{h}", align_bytes=256) for h in range(HALVES)]
-
-        def round_in_runs(copy, grouped, raw):
-            copy(grouped.rearrange("p (c i) j -> p c j i", i=RUN), raw.rearrange("p j (c i) -> p c j i", i=RUN))
-
-        def quantise(h, lo, grouped):
-            nc.vector.quantize_mx(
-                out=q_words[h][:, lo : lo + Q_PIECE].bitcast(FP8X4),
-                scales=q_scales[h][:, lo : lo + Q_PIECE],
-                in_=grouped.rearrange("p c j -> p (c j)"),
-            )
-
-        round_in_runs(nc.scalar.copy, grouped_first[:, :Q_PIECE, :], q_raw[0][:, :, :Q_PIECE])
-        round_in_runs(nc.scalar.copy, grouped_first[:, Q_PIECE:SCALAR_FIRST, :], q_raw[0][:, :, Q_PIECE:SCALAR_FIRST])
+        round_in_runs(nc.scalar.copy, 1, 0, Q_PIECE)
+        round_in_runs(nc.scalar.copy, 1, Q_PIECE, SCALAR_SHARE)
         nc.gpsimd.tensor_scalar(
-            grouped_first[:, SCALAR_FIRST:, :],
-            q_raw[0][:, :, SCALAR_FIRST:].rearrange("p j c -> p c j"),
+            grouped[1][:, SCALAR_SHARE:, :],
+            q_raw[1][:, :, SCALAR_SHARE:].rearrange("p j c -> p c j"),
             1.0,
             0.0,
             ALU.mult,
             ALU.add,
         )
-        quantise(0, 0, grouped_first[:, :Q_PIECE, :])
-        quantise(0, Q_PIECE, grouped_first[:, Q_PIECE:, :])
-        round_in_runs(nc.scalar.copy, grouped_last[:, :Q_PIECE, :], q_raw[1][:, :, :Q_PIECE])
-        round_in_runs(nc.vector.tensor_copy, grouped_last[:, Q_PIECE:, :], q_raw[1][:, :, Q_PIECE:])
-        quantise(1, 0, grouped_last[:, :Q_PIECE, :])
-        quantise(1, Q_PIECE, grouped_last[:, Q_PIECE:, :])
+        quantise(1, 0)
+        quantise(1, Q_PIECE)
 
         for h, lo, hi in STORES:
             squared = pool.tile([P, hi - lo], F32, name=f"squared{h}_{lo}", align_bytes=256)
@@ -112,7 +113,7 @@ def tile_attend_neu_relu2_srt_kernel(tc, qT, k_words, k_scales, offs, out):
                     out=acc[:],
                     lhsT=q_words[h][:].bitcast(FP8X4),
                     lhsT_scale=q_scales[h][:],
-                    rhs=key_words[:, at : at + WIDTH].bitcast(FP8X4),
+                    rhs=key_words[at // PICK][:, at % PICK : at % PICK + WIDTH].bitcast(FP8X4),
                     rhs_scale=key_scales[:, at : at + WIDTH],
                     start=True,
                     stop=True,

@@ -26,7 +26,7 @@ RUN = 4
 WIDTH = 128
 Q_PIECE = 64
 SCALAR_SHARE = 80
-STORES = ((0, 0, 256), (0, 256, 512), (1, 0, 128), (1, 128, 384), (1, 384, 512))
+STORES = ((0, 0, 256), (0, 256, 512), (1, 0, 128), (1, 128, 256), (1, 256, 512))
 
 
 def tile_attend_neu_relu2_srt_kernel(tc, qT, k_words, k_scales, offs, out):

@@ -66,6 +66,9 @@ def tile_attend_neu_relu2_srt_kernel(tc, qT, k_words, k_scales, offs, out):
                 q_raw[h][:, :, lo:hi].rearrange("p j (c i) -> p c j i", i=RUN),
             )
 
+        def gpsimd_copy(into, raw):
+            nc.gpsimd.tensor_scalar(into, raw, 1.0, 0.0, ALU.mult, ALU.add)
+
         def quantise(h, lo):
             nc.vector.quantize_mx(
                 out=q_words[h][:, lo : lo + Q_PIECE].bitcast(FP8X4),
@@ -94,14 +97,7 @@ def tile_attend_neu_relu2_srt_kernel(tc, qT, k_words, k_scales, offs, out):
 
         round_in_runs(nc.scalar.copy, 1, 0, Q_PIECE)
         round_in_runs(nc.scalar.copy, 1, Q_PIECE, SCALAR_SHARE)
-        nc.gpsimd.tensor_scalar(
-            grouped[1][:, SCALAR_SHARE:, :],
-            q_raw[1][:, :, SCALAR_SHARE:].rearrange("p j c -> p c j"),
-            1.0,
-            0.0,
-            ALU.mult,
-            ALU.add,
-        )
+        round_in_runs(gpsimd_copy, 1, SCALAR_SHARE, P)
         quantise(1, 0)
         quantise(1, Q_PIECE)
 

@@ -9,7 +9,6 @@ U32 = mybir.dt.uint32
 U16 = mybir.dt.uint16
 U8 = mybir.dt.uint8
 FP8X4 = mybir.dt.float8_e4m3fn_x4
-ACT = mybir.ActivationFunctionType
 ALU = mybir.AluOpType
 
 P = 128
@@ -115,6 +114,8 @@ def tile_attend_neu_relu2_srt_kernel(tc, qT, k_words, k_scales, offs, out):
                     stop=True,
                 )
                 rect = pool.tile([P, WIDTH], F32, name=f"rect{h}_{at}")
-                nc.scalar.activation(rect[:], acc[:], ACT.Relu)
-                nc.vector.tensor_tensor(squared[:, at - lo : at - lo + WIDTH], rect[:], rect[:], ALU.mult)
+                nc.scalar.copy(rect[:], acc[:])
+                nc.vector.scalar_tensor_tensor(
+                    squared[:, at - lo : at - lo + WIDTH], rect[:], 0.0, rect[:], ALU.max, ALU.mult
+                )
             nc.sync.dma_start(out[0, h * P : (h + 1) * P, lo:hi], squared[:])

from contextlib import ExitStack

import concourse.mybir as mybir

F32 = mybir.dt.float32
BF16 = mybir.dt.bfloat16
I32 = mybir.dt.int32
U32 = mybir.dt.uint32
U16 = mybir.dt.uint16
U8 = mybir.dt.uint8
FP8X4 = mybir.dt.float8_e4m3fn_x4
ALU = mybir.AluOpType

P = 128
PACK = 4
D, T, N, NQ = 512, 4096, 512, 256
FLOPS = 2 * NQ * N * D
HALVES = NQ // P
QUADS, QUAD = 4, 32
QUAD_ROWS = 4
SPREAD_FIRST, SPREAD_STEP = 32, 4
HEAD_COLS = 768
PICK = 256
RUN = 4
WIDTH = 128
Q_PIECE = 64
SCALAR_SHARE = 80
STORES = ((0, 0, 256), (0, 256, 512), (1, 0, 128), (1, 128, 256), (1, 256, 512))


def tile_attend_neu_relu2_srt_kernel(tc, qT, k_words, k_scales, offs, out):
    nc = tc.nc
    with ExitStack() as ctx:
        pool = ctx.enter_context(tc.tile_pool(name="held", bufs=1))
        psum = ctx.enter_context(tc.psum_pool(name="psum", bufs=1))

        table_scales = pool.tile([P, T], U8, name="table_scales", align_bytes=256)
        nc.vector.memset(table_scales[:].bitcast(I32), 0)
        key_scales = pool.tile([P, N], U8, name="key_scales", align_bytes=256)
        nc.vector.memset(key_scales[:].bitcast(I32), 0)

        table_words = pool.tile([P, T], I32, name="table_words", align_bytes=256)
        words_hbm = k_words[0].rearrange("p n t -> p (n t)").bitcast(I32)
        head_words = pool.tile([P, HEAD_COLS], I32, name="head_words", align_bytes=256)
        nc.sync.dma_start(head_words[:], words_hbm[:, :HEAD_COLS])
        q_hbm = qT[0].rearrange("(p j) c -> p j c", j=PACK)
        q_raw = [pool.tile([P, PACK, P], F32, name=f"q_raw{h}", align_bytes=256) for h in range(HALVES)]
        nc.sync.dma_start(q_raw[0][:], q_hbm[:, :, :P])
        offsets = pool.tile([P, N // 16], U16, name="offsets")
        nc.sync.dma_start(offsets[:], offs)
        spread_end = SPREAD_FIRST + SPREAD_STEP * QUADS * QUAD_ROWS
        nc.sync.dma_start(table_scales[SPREAD_FIRST:spread_end:SPREAD_STEP, :].bitcast(I32), k_scales[0].bitcast(I32))
        nc.sync.dma_start(table_words[:, HEAD_COLS:], words_hbm[:, HEAD_COLS:])
        nc.sync.dma_start(q_raw[1][:], q_hbm[:, :, P:])

        nc.vector.tensor_copy(table_words[:, :HEAD_COLS], head_words[:])

        grouped = [pool.tile([P, P, PACK], BF16, name=f"grouped{h}", align_bytes=256) for h in range(HALVES)]
        q_words = [pool.tile([P, P], U32, name=f"q_words{h}", align_bytes=256) for h in range(HALVES)]
        q_scales = [pool.tile([P, P], U8, name=f"q_scales{h}", align_bytes=256) for h in range(HALVES)]

        def round_in_runs(copy, h, lo, hi):
            copy(
                grouped[h][:, lo:hi, :].rearrange("p (c i) j -> p c j i", i=RUN),
                q_raw[h][:, :, lo:hi].rearrange("p j (c i) -> p c j i", i=RUN),
            )

        def gpsimd_copy(into, raw):
            nc.gpsimd.tensor_scalar(into, raw, 1.0, 0.0, ALU.mult, ALU.add)

        def quantise(h, lo):
            nc.vector.quantize_mx(
                out=q_words[h][:, lo : lo + Q_PIECE].bitcast(FP8X4),
                scales=q_scales[h][:, lo : lo + Q_PIECE],
                in_=grouped[h][:, lo : lo + Q_PIECE, :].rearrange("p c j -> p (c j)"),
            )

        round_in_runs(nc.scalar.copy, 0, 0, Q_PIECE)
        round_in_runs(nc.vector.tensor_copy, 0, Q_PIECE, P)

        picked_scales = pool.tile([P, N], U8, name="picked_scales", align_bytes=256)
        nc.vector.tensor_copy(picked_scales[:], table_scales[:].indirect(offsets[:]))
        for quad in range(QUADS):
            first = SPREAD_FIRST + SPREAD_STEP * QUAD_ROWS * quad
            nc.scalar.dma_start(
                key_scales[QUAD * quad : QUAD * quad + QUAD_ROWS, :].bitcast(I32),
                picked_scales[first : first + SPREAD_STEP * QUAD_ROWS : SPREAD_STEP, :].bitcast(I32),
            )
        quantise(0, 0)
        quantise(0, Q_PIECE)

        key_words = [pool.tile([P, PICK], U32, name=f"key_words{g}", align_bytes=256) for g in range(N // PICK)]
        for g in range(N // PICK):
            picks = offsets[:, g * PICK // 16 : (g + 1) * PICK // 16]
            nc.vector.tensor_copy(key_words[g][:], table_words[:].bitcast(U32).indirect(picks))

        round_in_runs(nc.scalar.copy, 1, 0, Q_PIECE)
        round_in_runs(nc.scalar.copy, 1, Q_PIECE, SCALAR_SHARE)
        round_in_runs(gpsimd_copy, 1, SCALAR_SHARE, P)
        quantise(1, 0)
        quantise(1, Q_PIECE)

        for h, lo, hi in STORES:
            squared = pool.tile([P, hi - lo], F32, name=f"squared{h}_{lo}", align_bytes=256)
            for at in range(lo, hi, WIDTH):
                acc = psum.tile([P, WIDTH], F32, name=f"acc{h}_{at}")
                nc.tensor.matmul_mx(
                    out=acc[:],
                    lhsT=q_words[h][:].bitcast(FP8X4),
                    lhsT_scale=q_scales[h][:],
                    rhs=key_words[at // PICK][:, at % PICK : at % PICK + WIDTH].bitcast(FP8X4),
                    rhs_scale=key_scales[:, at : at + WIDTH],
                    start=True,
                    stop=True,
                )
                rect = pool.tile([P, WIDTH], F32, name=f"rect{h}_{at}")
                nc.scalar.copy(rect[:], acc[:])
                nc.vector.scalar_tensor_tensor(
                    squared[:, at - lo : at - lo + WIDTH], rect[:], 0.0, rect[:], ALU.max, ALU.mult
                )
            nc.sync.dma_start(out[0, h * P : (h + 1) * P, lo:hi], squared[:])
